import numpy as np, ml_dtypes
CORES = [97,101,225,229,353,357,481,485]
N = 8
S, T = 8192, 1024
def entries(a): return a.T.reshape(-1)
def pack(v, P): return np.ascontiguousarray(np.asarray(v, np.int32).reshape(-1, P).T)
def lists(rng, how):
    M = rng.integers(0, S, (N, S)); b = rng.integers(0, S, T)
    if how == "alike": M = np.stack([rng.permutation(S) for f in range(N)]); b[:] = rng.integers(S)
    if how == "edge":
        M = np.where(rng.random((N, S)) < 0.5, 0, S - 1); w = rng.permutation(N) % 2 * (S - 1); M[:, 0] = w; M[:, S - 1] = S - 1 - w
        b = np.where(rng.random(T) < 0.5, 0, S - 1); b[rng.permutation(T)[:2]] = [0, S - 1]
    if how == "fold":
        V = np.stack([rng.permutation(S)[:4] for f in range(N + 1)]); M = V[np.arange(N)[:, None], rng.integers(0, 4, (N, S))]
        M[np.arange(N)[:, None], V[1:]] = V[:N]; b[rng.permutation(T)[:4]] = V[N]
    if how == "mixed":
        k = np.concatenate([[3, 3], rng.permutation(np.arange(N - 2) % 3)])
        for f in range(N): M[f] = [np.arange(S), rng.permutation(S), M[f], rng.integers(0, S, 4)[rng.integers(0, 4, S)]][k[f]]
    if how == "turn": M = np.stack([rng.permutation(S) for f in range(N)]); b = rng.permutation(S)[:T]
    return {"bp": np.stack([pack(m, 16) for m in M]), "st": np.broadcast_to(pack(b, 16), (N, 16, T // 16)).copy()}
def setup_inputs(rng):
    return dict({"tab": rng.standard_normal((N, 128, S), dtype=np.float32).astype(ml_dtypes.bfloat16)}, **lists(rng, "uniform"))
def setup_inputs_alike(rng):
    d = setup_inputs(rng); d.update(lists(rng, "alike"))
    for k in ("tab",): d[k] = (d[k].astype(np.float32) * 1048576.0).astype(d[k].dtype)
    return d
def setup_inputs_edge(rng):
    d = setup_inputs(rng); d.update(lists(rng, "edge"))
    for k in ("tab",): d[k] = (d[k].astype(np.float32) * (1 / 1024.0)).astype(d[k].dtype)
    return d
def setup_inputs_fold(rng):
    d = setup_inputs(rng); d.update(lists(rng, "fold"))
    return d
def setup_inputs_mixed(rng):
    d = setup_inputs(rng); d.update(lists(rng, "mixed"))
    return d
def setup_inputs_turn(rng):
    d = setup_inputs(rng); d.update(lists(rng, "turn"))
    return d
def check_inputs(x):
    bad = []
    if x["bp"].min() < 0 or x["bp"].max() >= S: bad.append("bp out of range")
    if x["st"].min() < 0 or x["st"].max() >= S: bad.append("st out of range")
    if not all(np.array_equal(a, x["st"][0]) for a in x["st"]): bad.append("st isn't alike on all ranks")
    return bad
def reference(tab, bp, st):
    b = entries(st[0]); y = np.zeros((N, 128, T), tab.dtype)
    for f in range(N - 1, -1, -1):
        y[f] = tab[f][:, b]
        b = entries(bp[f])[b]
    return {"y": y}

@@ -1,0 +1,272 @@
+from concourse.bass import DstId, RemoteDMATransfer
+from concourse.mybir import AluOpType as A, ActivationFunctionType as F
+
+N = 8
+SCRATCH = {
+    "bpi": ("sbuf", [128, 64], "int32"), "bpk": ("sbuf", [128, 64], "int32"), "bpc": ("sbuf", [128, 64], "int32"),
+    "pay": ("sbuf", [128, 128], "bfloat16"),
+    "sti": ("sbuf", [128, 8], "int32"), "stk": ("sbuf", [128, 8], "int32"), "stc": ("sbuf", [128, 8], "int32"),
+    "stkf": ("sbuf", [128, 8], "float32"), "stf": ("sbuf", [128, 64], "int32"),
+    "tabs": ("sbuf", [128, 8192], "bfloat16"), "yb": ("sbuf", [128, 1024], "bfloat16"),
+    "ia": ("sbuf", [128, 320], "int32"), "ib": ("sbuf", [128, 320], "int32"),
+    "ja": ("sbuf", [128, 136], "int32"), "jb": ("sbuf", [128, 136], "int32"), "ie": ("sbuf", [128, 128], "int32"),
+    "cst": ("sbuf", [128, 320], "bfloat16"), "dg": ("sbuf", [128, 128], "bfloat16"),
+    "dg16": ("sbuf", [128, 128], "bfloat16"), "rs": ("sbuf", [128, 128], "bfloat16"),
+    "ee": ("sbuf", [128, 1024], "bfloat16"), "rc": ("sbuf", [128, 1], "float32"),
+    "x0": ("sbuf", [128, 128], "bfloat16"), "sp": ("sbuf", [128, 128], "bfloat16"),
+    "foff": ("sbuf", [128, 64], "uint16"),
+    "repc": ("psum", [128, 512], "float32"), "repk": ("psum", [128, 512], "float32"),
+    "land": ("sbuf", [128, 128 * N], "bfloat16"),
+    "wc": ("sbuf", [128, 512 * N], "bfloat16"), "wk": ("sbuf", [128, 512 * N], "bfloat16"),
+}
+for _i in range(2):
+    for _n in ("xc", "xk", "z", "zs", "sel"):
+        SCRATCH["%s%d" % (_n, _i)] = ("sbuf", [128, 128], "bfloat16")
+    SCRATCH["off%d" % _i] = ("sbuf", [128, 8], "uint16")
+NB = 3
+for _i in range(NB):
+    SCRATCH["pc%d" % _i] = ("psum", [128, 512], "float32")
+    SCRATCH["pk%d" % _i] = ("psum", [128, 512], "float32")
+SEMAPHORES = ["v", "p", "s", "gi", "sent", "rsent", "bpl", "stl", "tab0", "tab1", "y0", "y1", "y2", "y3"] + \
+             ["a%d" % m for m in range(1, N)]
+
+
+def plan(topo, C):
+    first, relay = {}, {r: [] for r in range(N)}
+    for f in range(N):
+        direct = [r for r in range(f) if topo.may_write(C[f], C[r])]
+        far = [r for r in range(f) if r not in direct]
+        calls, rest = [], direct
+        if far:
+            via = max(r for r in direct if topo.host(C[r]) != topo.host(C[f]) and topo.die(C[r]) == topo.die(C[f])
+                      and all(topo.may_write(C[r], C[d]) for d in far))
+            relay[via].append((f, far))
+            calls.append([via])
+            rest = [r for r in direct if r != via]
+        if rest:
+            calls.append(rest)
+        first[f] = calls
+    return first, relay
+
+
+ORDER = {
+    0: "bv1 bv7 bs6 s7 c3 s6 k3 bv5 bs4 s5 c2 s4 k2 s3 s2 s1",
+    1: "bv7 bs6 s7 c3 s6 k3 bv5 bs4 s5 c2 s4 k2 s3 s2",
+    2: "bv5 bv4 bv3 bv7 bs6 s7 s6 s5 s4 s3",
+    3: "bv5 bv4 bv7 bs6 s7 s6 s5 s4",
+    4: "bv6 bv7 s7 c5 s6 k5 s5",
+    5: "bv7 bs6 s7 s6",
+    6: "bv7 s7",
+    7: "",
+}
+TABA = [8192, 4096, 4096, 4096, 3072, 3072, 3072, 3072]
+
+
+def rank_program(g, core, T, topo):
+    f = T.rank_of(core)
+    if f is None:
+        return
+    C = T.cores
+    first, relay = plan(topo, C)
+    V = g.vector
+    Q = {"v": V, "p": g.tensor, "s": g.scalar, "g": g, "y": g.sync}
+    cnt, seen = {}, {}
+
+    def need(q, *toks):
+        for tok in toks:
+            if tok is not None and seen.get((q, tok[0]), 0) < tok[1]:
+                Q[q].wait_ge(T.sem[tok[0]], tok[1])
+                seen[(q, tok[0])] = tok[1]
+
+    def inc(ins, sem, n=1):
+        ins.then_inc(T.sem[sem], n)
+        cnt[sem] = cnt.get(sem, 0) + n
+        return (sem, cnt[sem])
+
+    has_map, chain = f > 0, f < N - 1
+    bpl = inc(g.sync.dma_start(T.bpi[:, :], T.bp[:, :]), "bpl", 16) if has_map else None
+    for k in range(8):
+        if chain:
+            stl = inc(g.scalar.dma_start(T.sti[16 * k:16 * k + 16, :], T.st[:, 8 * k:8 * k + 8]), "stl", 16)
+        else:
+            stl = inc(g.scalar.dma_start(T.stf[16 * k:16 * k + 16, :], T.st[:, :]), "stl", 16)
+    ta = TABA[f]
+    tab0 = inc(g.sync.dma_start(T.tabs[:, 0:ta], T.tab[:, 0:ta]), "tab0", 16)
+
+    if chain:
+        gi = [inc(g.iota(T.ie[:, :], [[0, 8], [-8, 16]], 0, 1), "gi"),
+              inc(g.iota(T.ia[:, 0:128], [[-16, 8], [0, 16]], 0, 1), "gi"),
+              inc(g.iota(T.ia[:, 128:192], [[-16, 8], [0, 8]], 0, 1), "gi"),
+              inc(g.iota(T.ia[:, 192:320], [[0, 16], [-16, 8]], 0, 1), "gi"),
+              inc(g.iota(T.ja[:, 0:128], [[0, 8], [-1, 16]], 16, 1), "gi"),
+              inc(g.iota(T.ja[:, 128:136], [[0, 8]], 0, 1), "gi")]
+    c = {}
+
+    def constants():
+        need("v", gi[0])
+        for h in range(8):
+            c["ee"] = inc(V.tensor_scalar(T.ee[:, 128 * h:128 * h + 128], T.ie[:, :], float(h), None, A.is_equal), "v")
+        need("v", gi[-1])
+        a = inc(V.tensor_scalar(T.jb[:, :], T.ja[:, :], 15, None, A.bitwise_and), "v")
+        b = inc(V.tensor_scalar(T.ib[:, :], T.ia[:, :], 4, None, A.arith_shift_right), "v")
+        o = inc(V.memset(T.rs[:, :], 1.0), "v")
+        need("v", a)
+        c["dg"] = inc(V.tensor_scalar(T.dg[:, :], T.jb[:, 0:128], 0.0, None, A.is_equal), "v")
+        c["rc"] = inc(V.tensor_copy(T.rc[:, :], T.jb[:, 128:129]), "v")
+        need("v", b)
+        c["cst"] = inc(V.tensor_scalar(T.cst[:, :], T.ib[:, :], 0.0, None, A.is_equal), "v")
+        need("v", o)
+        c["rs"] = inc(V.memset(T.rs[:, 0:128:16], 0.0), "v")
+        need("v", c["dg"])
+        c["dg16"] = inc(V.tensor_scalar(T.dg16[:, :], T.dg[:, :], 16.0, None, A.mult), "v")
+
+    def encode():
+        need("v", bpl)
+        a = inc(V.tensor_scalar(T.bpk[:, :], T.bpi[:, :], 15, None, A.bitwise_and), "v")
+        b = inc(V.tensor_scalar(T.bpc[:, :], T.bpi[:, :], 4, None, A.arith_shift_right), "v")
+        need("v", a)
+        inc(V.tensor_copy(T.pay[:, 64:128], T.bpk[:, :]), "v")
+        need("v", b)
+        return inc(V.tensor_scalar(T.pay[:, 0:64], T.bpc[:, :], -256.0, None, A.add), "v")
+
+    early = f < N // 2
+    if chain and early:
+        constants()
+    enc = encode() if has_map else None
+    if chain and not early:
+        constants()
+
+    mask = topo.mask(C[1], C[0])
+    for a in C:
+        for b in C:
+            if topo.may_write(a, b) and a != b:
+                mask &= topo.mask(a, b)
+    ne = bin(mask).count("1")
+
+    def send(m, src, dsts, sem):
+        land = T.land[:, 128 * m:128 * m + 128]
+        ad = [topo.addr(C[d], core) for d in dsts]
+        if len(dsts) == 1:
+            g.remote_dma(out_ap=land, in_ap=src, remote_sem=T.sem["a%d" % m], local_sem=T.sem[sem],
+                         pid=ad[0][1], routing_id=ad[0][0], dma_engine_mask=mask)
+        else:
+            g.remote_dma_fused([RemoteDMATransfer(
+                dst_ids=[DstId(rid=r, pnc=p) for r, p in ad], dma_engine_mask=mask, remote_sem=T.sem["a%d" % m],
+                srcs=[src], dsts=[land] * len(dsts))], local_sem=T.sem[sem])
+        cnt[sem] = cnt.get(sem, 0) + ne
+        return (sem, cnt[sem])
+
+    def arrived(m):
+        return ("a%d" % m, ne)
+
+    done = None
+    for call in first[f]:
+        need("g", enc)
+        done = send(f, T.pay[:, :], call, "sent")
+    for m, dsts in relay[f]:
+        need("g", arrived(m))
+        done = send(m, T.land[:, 128 * m:128 * m + 128], dsts, "rsent")
+
+    tab1 = None
+    if ta < 8192:
+        need("y", done)
+        tab1 = inc(g.sync.dma_start(T.tabs[:, ta:8192], T.tab[:, ta:8192]), "tab1", 16)
+
+    G, GT, MQ = T.cst[:, 0:128], T.cst[:, 128:192], T.cst[:, 192:320]
+    ring, win = {"c": [], "k": []}, {}
+
+    def plane(m, w, q):
+        slot = len(ring[w]) % NB
+        need("p", arrived(m), c["ee"])
+        if len(ring[w]) >= NB:
+            need("p", win[(ring[w][-NB], w)])
+        ring[w].append(m)
+        ps, dst = T["p%s%d" % (w, slot)], T["w" + w][:, 512 * m:512 * m + 512]
+        col = 128 * m + (0 if w == "c" else 64)
+        for h in range(8):
+            t = inc(g.tensor.matmul(ps[:, 64 * h:64 * h + 64], T.ee[:, 128 * h:128 * h + 128],
+                                    T.land[:, col:col + 64], True, True), "p")
+        need(q, t)
+        if q == "v":
+            win[(m, w)] = inc(V.tensor_copy(dst, ps[:, :]), "v")
+        else:
+            win[(m, w)] = inc(g.scalar.activation(dst, ps[:, :], F.Copy), "s")
+
+    if chain:
+        need("v", stl)
+        a = inc(V.tensor_scalar(T.stk[:, :], T.sti[:, :], 15, None, A.bitwise_and), "v")
+        b = inc(V.tensor_scalar(T.stc[:, :], T.sti[:, :], 4, None, A.arith_shift_right), "v")
+        need("v", a)
+        a = inc(V.tensor_copy(T.stkf[:, :], T.stk[:, :]), "v")
+        need("v", b)
+        off = inc(V.tensor_copy(T.off0[:, :], T.stc[:, :]), "v")
+        need("v", a, c["dg"])
+        for q in range(8):
+            t = inc(V.tensor_scalar(T.x0[:, 16 * q:16 * q + 16], T.dg[:, 16 * q:16 * q + 16],
+                                    T.stkf[:, q:q + 1], None, A.mult), "v")
+        need("p", t, c["cst"])
+        t = inc(g.tensor.matmul(T.repk[:, 0:128], G, T.x0[:, :], True, True), "p")
+        need("v", t, c["rc"])
+        sel = inc(V.tensor_scalar(T.sel0[:, :], T.repk[:, 0:128], T.rc[:, 0:1], None, A.is_equal), "v")
+        par = 0
+        for word in ORDER[f].split():
+            m = int(word[-1])
+            if word[0] == "b":
+                plane(m, "c", "s")
+                plane(m, "k", word[1])
+                continue
+            if word[0] in "ck":
+                plane(m, word[0], "s")
+                continue
+            xc, xk = T["xc%d" % par], T["xk%d" % par]
+            offs, sl = T["off%d" % par][:, 0:8], T["sel%d" % par][:, :]
+            need("v", off, sel, win[(m, "c")])
+            tc = inc(V.tensor_tensor(xc[:, :], T.wc[:, 512 * m:512 * m + 512].indirect(offs), sl, A.mult), "v")
+            need("v", win[(m, "k")])
+            tk = inc(V.tensor_tensor(xk[:, :], T.wk[:, 512 * m:512 * m + 512].indirect(offs), sl, A.mult), "v")
+            if m == f + 1:
+                break
+            need("p", tc)
+            rc_ = inc(g.tensor.matmul(T.repc[:, 0:128], G, xc[:, :], True, True), "p")
+            need("p", tk)
+            rk_ = inc(g.tensor.matmul(T.repk[:, 0:128], G, xk[:, :], True, True), "p")
+            z, zs, par = T["z%d" % par], T["zs%d" % par], 1 - par
+            need("v", rc_)
+            t = inc(V.tensor_tensor(z[:, :], T.repc[:, 0:128], T.dg[:, :], A.mult), "v")
+            need("v", t, c["rs"])
+            t = inc(V.tensor_tensor_scan(zs[:, :], T.rs[:, :], z[:, :], 0.0, A.mult, A.add), "v")
+            need("v", rk_)
+            sel = inc(V.tensor_scalar(T["sel%d" % par][:, :], T.repk[:, 0:128], T.rc[:, 0:1], None, A.is_equal), "v")
+            need("v", t)
+            off = inc(V.tensor_scalar(T["off%d" % par][:, :], zs[:, 15:128:16], 256.0, None, A.add), "v")
+        need("p", tc, c["cst"])
+        inc(g.tensor.matmul(T.repc[:, 0:64], xc[:, :], GT, True, True), "p")
+        need("p", tk)
+        t = inc(g.tensor.matmul(T.repc[:, 64:128], xk[:, :], GT, True, True), "p")
+        need("v", t)
+        t = inc(V.tensor_tensor(T.sp[:, :], T.repc[:, 0:128], MQ, A.mult), "v")
+        need("p", t, c["dg16"])
+        g.tensor.matmul(T.repk[:, 0:64], T.dg16[:, :], T.sp[:, 0:64], True, False)
+        t = inc(g.tensor.matmul(T.repk[:, 0:64], T.dg[:, :], T.sp[:, 64:128], False, True), "p")
+        need("v", t)
+        t = inc(V.tensor_scalar(T.foff[:, :], T.repk[:, 0:64], 4096.0, None, A.add), "v")
+    else:
+        need("v", stl)
+        t = inc(V.tensor_copy(T.foff[:, :], T.stf[:, :]), "v")
+
+    need("v", t, tab0, tab1)
+    need("s", t, tab0, tab1)
+    tq = {}
+    for i in (0, 2, 1, 3):
+        src = T.tabs[:, :].indirect(T.foff[:, 16 * i:16 * i + 16])
+        dst = T.yb[:, 256 * i:256 * i + 256]
+        tq[i] = inc(V.tensor_copy(dst, src), "v") if i < 2 else inc(g.scalar.activation(dst, src, F.Copy), "s")
+    for i in (0, 2, 1, 3):
+        q, eng = ("s", g.scalar) if i == 3 else ("y", g.sync)
+        need(q, tq[i])
+        inc(eng.dma_start(T.y[:, 256 * i:256 * i + 256], T.yb[:, 256 * i:256 * i + 256]), "y%d" % i, 16)
+
+    for s in sorted(cnt):
+        need("g", (s, cnt[s]))
+    for m in range(f + 1, N):
+        need("g", arrived(m))

@@ -11,7 +11,7 @@ SCRATCH = {
     "ia": ("sbuf", [128, 320], "int32"), "ib": ("sbuf", [128, 320], "int32"),
     "ja": ("sbuf", [128, 136], "int32"), "jb": ("sbuf", [128, 136], "int32"), "ie": ("sbuf", [128, 128], "int32"),
     "cst": ("sbuf", [128, 320], "bfloat16"), "dg": ("sbuf", [128, 128], "bfloat16"),
-    "dg16": ("sbuf", [128, 128], "bfloat16"), "rs": ("sbuf", [128, 128], "bfloat16"),
+    "dg16": ("sbuf", [128, 128], "bfloat16"), "rs": ("sbuf", [128, 128], "bfloat16"), "nd": ("sbuf", [128, 128], "bfloat16"),
     "ee": ("sbuf", [128, 1024], "bfloat16"), "rc": ("sbuf", [128, 1], "float32"),
     "x0": ("sbuf", [128, 128], "bfloat16"), "sp": ("sbuf", [128, 128], "bfloat16"),
     "foff": ("sbuf", [128, 64], "uint16"),
@@ -20,14 +20,13 @@ SCRATCH = {
     "wc": ("sbuf", [128, 512 * N], "bfloat16"), "wk": ("sbuf", [128, 512 * N], "bfloat16"),
 }
 for _i in range(2):
-    for _n in ("xc", "xk", "z", "zs", "sel"):
+    for _n in ("xc", "xk", "zs", "sel"):
         SCRATCH["%s%d" % (_n, _i)] = ("sbuf", [128, 128], "bfloat16")
     SCRATCH["off%d" % _i] = ("sbuf", [128, 8], "uint16")
-NB = 3
+NB = 6
 for _i in range(NB):
-    SCRATCH["pc%d" % _i] = ("psum", [128, 512], "float32")
-    SCRATCH["pk%d" % _i] = ("psum", [128, 512], "float32")
-SEMAPHORES = ["v", "p", "s", "gi", "sent", "rsent", "bpl", "stl", "tab0", "tab1", "y0", "y1", "y2", "y3"] + \
+    SCRATCH["pw%d" % _i] = ("psum", [128, 512], "float32")
+SEMAPHORES = ["v", "p", "s", "gi", "sent", "rsent", "bpl", "stl", "tab0", "tab1", "y0", "y1", "y2"] + \
              ["a%d" % m for m in range(1, N)]
 
 
@@ -49,17 +48,30 @@ def plan(topo, C):
     return first, relay
 
 
+def whole(m, qc="s", qk="s"):
+    return "c%da%s k%da%s " % (m, qc, m, qk)
+
+
+def halves(m):
+    return "c%dlv c%dhs k%dlv k%dhv " % (m, m, m, m)
+
+
+def behind(m):
+    return "c%das k%dls k%dhw " % (m, m, m)
+
+
 ORDER = {
-    0: "bv1 bv7 bs6 s7 c3 s6 k3 bv5 bs4 s5 c2 s4 k2 s3 s2 s1",
-    1: "bv7 bs6 s7 c3 s6 k3 bv5 bs4 s5 c2 s4 k2 s3 s2",
-    2: "bv5 bv4 bv3 bv7 bs6 s7 s6 s5 s4 s3",
-    3: "bv5 bv4 bv7 bs6 s7 s6 s5 s4",
-    4: "bv6 bv7 s7 c5 s6 k5 s5",
-    5: "bv7 bs6 s7 s6",
-    6: "bv7 s7",
+    0: whole(1, "s", "v") + halves(7) + behind(6) + "s7 c3as k3as s6 " + halves(5) + behind(4) +
+       "s5 c2as s4 k2as s3 s2 s1",
+    1: halves(7) + behind(6) + "s7 c3as k3aw s6 " + halves(5) + behind(4) + "s5 c2as s4 k2as s3 s2",
+    2: whole(5, "s", "v") + whole(4, "s", "v") + whole(3, "s", "v") + halves(7) + behind(6) + "s7 s6 s5 s4 s3",
+    3: whole(5, "s", "v") + whole(4, "s", "v") + halves(7) + behind(6) + "s7 s6 s5 s4",
+    4: whole(6, "s", "v") + halves(7) + "s7 c5as s6 k5as s5",
+    5: halves(7) + behind(6) + "s7 s6",
+    6: halves(7) + "s7",
     7: "",
 }
-TABA = [8192, 4096, 4096, 4096, 3072, 3072, 3072, 3072]
+TABA = [8192, 1024, 3072, 3072, 3072, 3072, 2048, 2048]
 
 
 def rank_program(g, core, T, topo):
@@ -86,38 +98,38 @@ def rank_program(g, core, T, topo):
     has_map, chain = f > 0, f < N - 1
     bpl = inc(g.sync.dma_start(T.bpi[:, :], T.bp[:, :]), "bpl", 16) if has_map else None
     for k in range(8):
+        eng = (g.scalar, g.sync)[k % 2]
         if chain:
-            stl = inc(g.scalar.dma_start(T.sti[16 * k:16 * k + 16, :], T.st[:, 8 * k:8 * k + 8]), "stl", 16)
+            stl = inc(eng.dma_start(T.sti[16 * k:16 * k + 16, :], T.st[:, 8 * k:8 * k + 8]), "stl", 16)
         else:
-            stl = inc(g.scalar.dma_start(T.stf[16 * k:16 * k + 16, :], T.st[:, :]), "stl", 16)
+            stl = inc(eng.dma_start(T.stf[16 * k:16 * k + 16, :], T.st[:, :]), "stl", 16)
     ta = TABA[f]
     tab0 = inc(g.sync.dma_start(T.tabs[:, 0:ta], T.tab[:, 0:ta]), "tab0", 16)
 
+    c, gi = {}, {}
     if chain:
-        gi = [inc(g.iota(T.ie[:, :], [[0, 8], [-8, 16]], 0, 1), "gi"),
-              inc(g.iota(T.ia[:, 0:128], [[-16, 8], [0, 16]], 0, 1), "gi"),
-              inc(g.iota(T.ia[:, 128:192], [[-16, 8], [0, 8]], 0, 1), "gi"),
-              inc(g.iota(T.ia[:, 192:320], [[0, 16], [-16, 8]], 0, 1), "gi"),
-              inc(g.iota(T.ja[:, 0:128], [[0, 8], [-1, 16]], 16, 1), "gi"),
-              inc(g.iota(T.ja[:, 128:136], [[0, 8]], 0, 1), "gi")]
-    c = {}
+        gi["e"] = inc(g.iota(T.ie[:, :], [[0, 8], [-8, 16]], 0, 1), "gi")
+        inc(g.iota(T.ja[:, 0:128], [[0, 8], [-1, 16]], 16, 1), "gi")
+        gi["j"] = inc(g.iota(T.ja[:, 128:136], [[0, 8]], 0, 1), "gi")
+        gi["g"] = inc(g.iota(T.ia[:, 0:128], [[-16, 8], [0, 16]], 0, 1), "gi")
 
     def constants():
-        need("v", gi[0])
+        need("v", gi["e"])
         for h in range(8):
             c["ee"] = inc(V.tensor_scalar(T.ee[:, 128 * h:128 * h + 128], T.ie[:, :], float(h), None, A.is_equal), "v")
-        need("v", gi[-1])
+        need("v", gi["j"], gi["g"])
         a = inc(V.tensor_scalar(T.jb[:, :], T.ja[:, :], 15, None, A.bitwise_and), "v")
-        b = inc(V.tensor_scalar(T.ib[:, :], T.ia[:, :], 4, None, A.arith_shift_right), "v")
-        o = inc(V.memset(T.rs[:, :], 1.0), "v")
+        b = inc(V.tensor_scalar(T.ib[:, 0:128], T.ia[:, 0:128], 4, None, A.arith_shift_right), "v")
+        o = inc(V.memset(T.rs[:, :], 0.0), "v")
         need("v", a)
         c["dg"] = inc(V.tensor_scalar(T.dg[:, :], T.jb[:, 0:128], 0.0, None, A.is_equal), "v")
         c["rc"] = inc(V.tensor_copy(T.rc[:, :], T.jb[:, 128:129]), "v")
         need("v", b)
-        c["cst"] = inc(V.tensor_scalar(T.cst[:, :], T.ib[:, :], 0.0, None, A.is_equal), "v")
+        c["g"] = inc(V.tensor_scalar(T.cst[:, 0:128], T.ib[:, 0:128], 0.0, None, A.is_equal), "v")
         need("v", o)
-        c["rs"] = inc(V.memset(T.rs[:, 0:128:16], 0.0), "v")
+        c["rs"] = inc(V.memset(T.rs[:, 0:128:16], -4096.0), "v")
         need("v", c["dg"])
+        c["nd"] = inc(V.tensor_scalar(T.nd[:, :], T.dg[:, :], 1024.0, -1024.0, A.mult, A.add), "v")
         c["dg16"] = inc(V.tensor_scalar(T.dg16[:, :], T.dg[:, :], 16.0, None, A.mult), "v")
 
     def encode():
@@ -129,11 +141,8 @@ def rank_program(g, core, T, topo):
         need("v", b)
         return inc(V.tensor_scalar(T.pay[:, 0:64], T.bpc[:, :], -256.0, None, A.add), "v")
 
-    early = f < N // 2
-    if chain and early:
-        constants()
     enc = encode() if has_map else None
-    if chain and not early:
+    if chain:
         constants()
 
     mask = topo.mask(C[1], C[0])
@@ -163,6 +172,9 @@ def rank_program(g, core, T, topo):
     for call in first[f]:
         need("g", enc)
         done = send(f, T.pay[:, :], call, "sent")
+    if chain:
+        inc(g.iota(T.ia[:, 128:192], [[-16, 8], [0, 8]], 0, 1), "gi")
+        gi["l"] = inc(g.iota(T.ia[:, 192:320], [[0, 16], [-16, 8]], 0, 1), "gi")
     for m, dsts in relay[f]:
         need("g", arrived(m))
         done = send(m, T.land[:, 128 * m:128 * m + 128], dsts, "rsent")
@@ -173,24 +185,35 @@ def rank_program(g, core, T, topo):
         tab1 = inc(g.sync.dma_start(T.tabs[:, ta:8192], T.tab[:, ta:8192]), "tab1", 16)
 
     G, GT, MQ = T.cst[:, 0:128], T.cst[:, 128:192], T.cst[:, 192:320]
-    ring, win = {"c": [], "k": []}, {}
+    banks, win, later = [], {}, []
 
-    def plane(m, w, q):
-        slot = len(ring[w]) % NB
+    def copy(q, ps, dst):
+        if q == "s":
+            return inc(g.scalar.activation(dst, ps, F.Copy), "s")
+        return inc(V.tensor_copy(dst, ps), "v")
+
+    def plane(w, m, part, q):
+        hs = {"a": range(8), "l": range(4), "h": range(4, 8)}[part]
+        k, n = len(banks) % NB, 64 * len(hs)
         need("p", arrived(m), c["ee"])
-        if len(ring[w]) >= NB:
-            need("p", win[(ring[w][-NB], w)])
-        ring[w].append(m)
-        ps, dst = T["p%s%d" % (w, slot)], T["w" + w][:, 512 * m:512 * m + 512]
+        if len(banks) >= NB:
+            need("p", banks[-NB][0])
+        ps, at = T["pw%d" % k], 512 * m + 64 * hs[0]
         col = 128 * m + (0 if w == "c" else 64)
-        for h in range(8):
-            t = inc(g.tensor.matmul(ps[:, 64 * h:64 * h + 64], T.ee[:, 128 * h:128 * h + 128],
+        for x, h in enumerate(hs):
+            t = inc(g.tensor.matmul(ps[:, 64 * x:64 * x + 64], T.ee[:, 128 * h:128 * h + 128],
                                     T.land[:, col:col + 64], True, True), "p")
-        need(q, t)
-        if q == "v":
-            win[(m, w)] = inc(V.tensor_copy(dst, ps[:, :]), "v")
+        mine = [None]
+        banks.append(mine)
+
+        def out():
+            need("v" if q == "w" else q, t)
+            mine[0] = copy(q, ps[:, 0:n], T["w" + w][:, at:at + n])
+            win.setdefault((m, w), []).append(mine[0])
+        if q == "w":
+            later.append(out)
         else:
-            win[(m, w)] = inc(g.scalar.activation(dst, ps[:, :], F.Copy), "s")
+            out()
 
     if chain:
         need("v", stl)
@@ -204,40 +227,42 @@ def rank_program(g, core, T, topo):
         for q in range(8):
             t = inc(V.tensor_scalar(T.x0[:, 16 * q:16 * q + 16], T.dg[:, 16 * q:16 * q + 16],
                                     T.stkf[:, q:q + 1], None, A.mult), "v")
-        need("p", t, c["cst"])
+        need("p", t, c["g"], c["nd"])
         t = inc(g.tensor.matmul(T.repk[:, 0:128], G, T.x0[:, :], True, True), "p")
         need("v", t, c["rc"])
         sel = inc(V.tensor_scalar(T.sel0[:, :], T.repk[:, 0:128], T.rc[:, 0:1], None, A.is_equal), "v")
-        par = 0
+        need("v", gi["l"])
+        a = inc(V.tensor_scalar(T.ib[:, 128:320], T.ia[:, 128:320], 4, None, A.arith_shift_right), "v")
+        need("v", a)
+        c["cst"] = inc(V.tensor_scalar(T.cst[:, 128:320], T.ib[:, 128:320], 0.0, None, A.is_equal), "v")
+        par, scan = 0, None
         for word in ORDER[f].split():
-            m = int(word[-1])
-            if word[0] == "b":
-                plane(m, "c", "s")
-                plane(m, "k", word[1])
-                continue
-            if word[0] in "ck":
-                plane(m, word[0], "s")
+            m = int(word[1])
+            if word[0] != "s":
+                plane(word[0], m, word[2], word[3])
                 continue
             xc, xk = T["xc%d" % par], T["xk%d" % par]
             offs, sl = T["off%d" % par][:, 0:8], T["sel%d" % par][:, :]
-            need("v", off, sel, win[(m, "c")])
+            need("v", off, sel, *win[(m, "c")])
             tc = inc(V.tensor_tensor(xc[:, :], T.wc[:, 512 * m:512 * m + 512].indirect(offs), sl, A.mult), "v")
-            need("v", win[(m, "k")])
+            need("v", *win[(m, "k")])
             tk = inc(V.tensor_tensor(xk[:, :], T.wk[:, 512 * m:512 * m + 512].indirect(offs), sl, A.mult), "v")
             if m == f + 1:
                 break
+            need("p", scan)
+            g.tensor.matmul(T.repc[:, 0:128], T.dg[0:16, :], T.nd[0:16, :], True, False)
             need("p", tc)
-            rc_ = inc(g.tensor.matmul(T.repc[:, 0:128], G, xc[:, :], True, True), "p")
+            rc_ = inc(g.tensor.matmul(T.repc[:, 0:128], G, xc[:, :], False, True), "p")
             need("p", tk)
             rk_ = inc(g.tensor.matmul(T.repk[:, 0:128], G, xk[:, :], True, True), "p")
-            z, zs, par = T["z%d" % par], T["zs%d" % par], 1 - par
-            need("v", rc_)
-            t = inc(V.tensor_tensor(z[:, :], T.repc[:, 0:128], T.dg[:, :], A.mult), "v")
-            need("v", t, c["rs"])
-            t = inc(V.tensor_tensor_scan(zs[:, :], T.rs[:, :], z[:, :], 0.0, A.mult, A.add), "v")
+            while later:
+                later.pop(0)()
+            zs, par = T["zs%d" % par], 1 - par
+            need("v", rc_, c["rs"])
+            scan = inc(V.tensor_tensor_scan(zs[:, :], T.rs[:, :], T.repc[:, 0:128], 0.0, A.add, A.max), "v")
             need("v", rk_)
             sel = inc(V.tensor_scalar(T["sel%d" % par][:, :], T.repk[:, 0:128], T.rc[:, 0:1], None, A.is_equal), "v")
-            need("v", t)
+            need("v", scan)
             off = inc(V.tensor_scalar(T["off%d" % par][:, :], zs[:, 15:128:16], 256.0, None, A.add), "v")
         need("p", tc, c["cst"])
         inc(g.tensor.matmul(T.repc[:, 0:64], xc[:, :], GT, True, True), "p")
@@ -256,15 +281,16 @@ def rank_program(g, core, T, topo):
 
     need("v", t, tab0, tab1)
     need("s", t, tab0, tab1)
-    tq = {}
-    for i in (0, 2, 1, 3):
-        src = T.tabs[:, :].indirect(T.foff[:, 16 * i:16 * i + 16])
-        dst = T.yb[:, 256 * i:256 * i + 256]
-        tq[i] = inc(V.tensor_copy(dst, src), "v") if i < 2 else inc(g.scalar.activation(dst, src, F.Copy), "s")
-    for i in (0, 2, 1, 3):
-        q, eng = ("s", g.scalar) if i == 3 else ("y", g.sync)
-        need(q, tq[i])
-        inc(eng.dma_start(T.y[:, 256 * i:256 * i + 256], T.yb[:, 256 * i:256 * i + 256]), "y%d" % i, 16)
+    pieces = [(0, 256, "v"), (512, 1024, "s"), (256, 512, "v")]
+    toks = []
+    for lo, hi, q in pieces:
+        src = T.tabs[:, :].indirect(T.foff[:, lo // 16:hi // 16])
+        toks.append(copy(q, src, T.yb[:, lo:hi]))
+    for i in (0, 2, 1):
+        lo, hi, q = pieces[i]
+        need("s" if q == "s" else "y", toks[i])
+        eng = g.scalar if q == "s" else g.sync
+        inc(eng.dma_start(T.y[:, lo:hi], T.yb[:, lo:hi]), "y%d" % i, 16)
 
     for s in sorted(cnt):
         need("g", (s, cnt[s]))

from concourse.bass import DstId, RemoteDMATransfer
from concourse.mybir import AluOpType as A, ActivationFunctionType as F

N = 8
SCRATCH = {
    "bpi": ("sbuf", [128, 64], "int32"), "bpk": ("sbuf", [128, 64], "int32"), "bpc": ("sbuf", [128, 64], "int32"),
    "pay": ("sbuf", [128, 128], "bfloat16"),
    "sti": ("sbuf", [128, 8], "int32"), "stk": ("sbuf", [128, 8], "int32"), "stc": ("sbuf", [128, 8], "int32"),
    "stkf": ("sbuf", [128, 8], "float32"), "stf": ("sbuf", [128, 64], "int32"),
    "tabs": ("sbuf", [128, 8192], "bfloat16"), "yb": ("sbuf", [128, 1024], "bfloat16"),
    "ia": ("sbuf", [128, 320], "int32"), "ib": ("sbuf", [128, 320], "int32"),
    "ja": ("sbuf", [128, 136], "int32"), "jb": ("sbuf", [128, 136], "int32"), "ie": ("sbuf", [128, 128], "int32"),
    "cst": ("sbuf", [128, 320], "bfloat16"), "dg": ("sbuf", [128, 128], "bfloat16"),
    "dg16": ("sbuf", [128, 128], "bfloat16"), "rs": ("sbuf", [128, 128], "bfloat16"), "nd": ("sbuf", [128, 128], "bfloat16"),
    "ee": ("sbuf", [128, 1024], "bfloat16"), "rc": ("sbuf", [128, 1], "float32"),
    "x0": ("sbuf", [128, 128], "bfloat16"), "sp": ("sbuf", [128, 128], "bfloat16"),
    "foff": ("sbuf", [128, 64], "uint16"),
    "repc": ("psum", [128, 512], "float32"), "repk": ("psum", [128, 512], "float32"),
    "land": ("sbuf", [128, 128 * N], "bfloat16"),
    "wc": ("sbuf", [128, 512 * N], "bfloat16"), "wk": ("sbuf", [128, 512 * N], "bfloat16"),
}
for _i in range(2):
    for _n in ("xc", "xk", "zs", "sel"):
        SCRATCH["%s%d" % (_n, _i)] = ("sbuf", [128, 128], "bfloat16")
    SCRATCH["off%d" % _i] = ("sbuf", [128, 8], "uint16")
NB = 6
for _i in range(NB):
    SCRATCH["pw%d" % _i] = ("psum", [128, 512], "float32")
SEMAPHORES = ["v", "p", "s", "gi", "sent", "rsent", "bpl", "stl", "tab0", "tab1", "y0", "y1", "y2"] + \
             ["a%d" % m for m in range(1, N)]


def plan(topo, C):
    first, relay = {}, {r: [] for r in range(N)}
    for f in range(N):
        direct = [r for r in range(f) if topo.may_write(C[f], C[r])]
        far = [r for r in range(f) if r not in direct]
        calls, rest = [], direct
        if far:
            via = max(r for r in direct if topo.host(C[r]) != topo.host(C[f]) and topo.die(C[r]) == topo.die(C[f])
                      and all(topo.may_write(C[r], C[d]) for d in far))
            relay[via].append((f, far))
            calls.append([via])
            rest = [r for r in direct if r != via]
        if rest:
            calls.append(rest)
        first[f] = calls
    return first, relay


def whole(m, qc="s", qk="s"):
    return "c%da%s k%da%s " % (m, qc, m, qk)


def halves(m):
    return "c%dlv c%dhs k%dlv k%dhv " % (m, m, m, m)


def behind(m):
    return "c%das k%dls k%dhw " % (m, m, m)


ORDER = {
    0: whole(1, "s", "v") + halves(7) + behind(6) + "s7 c3as k3as s6 " + halves(5) + behind(4) +
       "s5 c2as s4 k2as s3 s2 s1",
    1: halves(7) + behind(6) + "s7 c3as k3aw s6 " + halves(5) + behind(4) + "s5 c2as s4 k2as s3 s2",
    2: whole(5, "s", "v") + whole(4, "s", "v") + whole(3, "s", "v") + halves(7) + behind(6) + "s7 s6 s5 s4 s3",
    3: whole(5, "s", "v") + whole(4, "s", "v") + halves(7) + behind(6) + "s7 s6 s5 s4",
    4: whole(6, "s", "v") + halves(7) + "s7 c5as s6 k5as s5",
    5: halves(7) + behind(6) + "s7 s6",
    6: halves(7) + "s7",
    7: "",
}
TABA = [8192, 1024, 3072, 3072, 3072, 3072, 2048, 2048]


def rank_program(g, core, T, topo):
    f = T.rank_of(core)
    if f is None:
        return
    C = T.cores
    first, relay = plan(topo, C)
    V = g.vector
    Q = {"v": V, "p": g.tensor, "s": g.scalar, "g": g, "y": g.sync}
    cnt, seen = {}, {}

    def need(q, *toks):
        for tok in toks:
            if tok is not None and seen.get((q, tok[0]), 0) < tok[1]:
                Q[q].wait_ge(T.sem[tok[0]], tok[1])
                seen[(q, tok[0])] = tok[1]

    def inc(ins, sem, n=1):
        ins.then_inc(T.sem[sem], n)
        cnt[sem] = cnt.get(sem, 0) + n
        return (sem, cnt[sem])

    has_map, chain = f > 0, f < N - 1
    bpl = inc(g.sync.dma_start(T.bpi[:, :], T.bp[:, :]), "bpl", 16) if has_map else None
    for k in range(8):
        eng = (g.scalar, g.sync)[k % 2]
        if chain:
            stl = inc(eng.dma_start(T.sti[16 * k:16 * k + 16, :], T.st[:, 8 * k:8 * k + 8]), "stl", 16)
        else:
            stl = inc(eng.dma_start(T.stf[16 * k:16 * k + 16, :], T.st[:, :]), "stl", 16)
    ta = TABA[f]
    tab0 = inc(g.sync.dma_start(T.tabs[:, 0:ta], T.tab[:, 0:ta]), "tab0", 16)

    c, gi = {}, {}
    if chain:
        gi["e"] = inc(g.iota(T.ie[:, :], [[0, 8], [-8, 16]], 0, 1), "gi")
        inc(g.iota(T.ja[:, 0:128], [[0, 8], [-1, 16]], 16, 1), "gi")
        gi["j"] = inc(g.iota(T.ja[:, 128:136], [[0, 8]], 0, 1), "gi")
        gi["g"] = inc(g.iota(T.ia[:, 0:128], [[-16, 8], [0, 16]], 0, 1), "gi")

    def constants():
        need("v", gi["e"])
        for h in range(8):
            c["ee"] = inc(V.tensor_scalar(T.ee[:, 128 * h:128 * h + 128], T.ie[:, :], float(h), None, A.is_equal), "v")
        need("v", gi["j"], gi["g"])
        a = inc(V.tensor_scalar(T.jb[:, :], T.ja[:, :], 15, None, A.bitwise_and), "v")
        b = inc(V.tensor_scalar(T.ib[:, 0:128], T.ia[:, 0:128], 4, None, A.arith_shift_right), "v")
        o = inc(V.memset(T.rs[:, :], 0.0), "v")
        need("v", a)
        c["dg"] = inc(V.tensor_scalar(T.dg[:, :], T.jb[:, 0:128], 0.0, None, A.is_equal), "v")
        c["rc"] = inc(V.tensor_copy(T.rc[:, :], T.jb[:, 128:129]), "v")
        need("v", b)
        c["g"] = inc(V.tensor_scalar(T.cst[:, 0:128], T.ib[:, 0:128], 0.0, None, A.is_equal), "v")
        need("v", o)
        c["rs"] = inc(V.memset(T.rs[:, 0:128:16], -4096.0), "v")
        need("v", c["dg"])
        c["nd"] = inc(V.tensor_scalar(T.nd[:, :], T.dg[:, :], 1024.0, -1024.0, A.mult, A.add), "v")
        c["dg16"] = inc(V.tensor_scalar(T.dg16[:, :], T.dg[:, :], 16.0, None, A.mult), "v")

    def encode():
        need("v", bpl)
        a = inc(V.tensor_scalar(T.bpk[:, :], T.bpi[:, :], 15, None, A.bitwise_and), "v")
        b = inc(V.tensor_scalar(T.bpc[:, :], T.bpi[:, :], 4, None, A.arith_shift_right), "v")
        need("v", a)
        inc(V.tensor_copy(T.pay[:, 64:128], T.bpk[:, :]), "v")
        need("v", b)
        return inc(V.tensor_scalar(T.pay[:, 0:64], T.bpc[:, :], -256.0, None, A.add), "v")

    enc = encode() if has_map else None
    if chain:
        constants()

    mask = topo.mask(C[1], C[0])
    for a in C:
        for b in C:
            if topo.may_write(a, b) and a != b:
                mask &= topo.mask(a, b)
    ne = bin(mask).count("1")

    def send(m, src, dsts, sem):
        land = T.land[:, 128 * m:128 * m + 128]
        ad = [topo.addr(C[d], core) for d in dsts]
        if len(dsts) == 1:
            g.remote_dma(out_ap=land, in_ap=src, remote_sem=T.sem["a%d" % m], local_sem=T.sem[sem],
                         pid=ad[0][1], routing_id=ad[0][0], dma_engine_mask=mask)
        else:
            g.remote_dma_fused([RemoteDMATransfer(
                dst_ids=[DstId(rid=r, pnc=p) for r, p in ad], dma_engine_mask=mask, remote_sem=T.sem["a%d" % m],
                srcs=[src], dsts=[land] * len(dsts))], local_sem=T.sem[sem])
        cnt[sem] = cnt.get(sem, 0) + ne
        return (sem, cnt[sem])

    def arrived(m):
        return ("a%d" % m, ne)

    done = None
    for call in first[f]:
        need("g", enc)
        done = send(f, T.pay[:, :], call, "sent")
    if chain:
        inc(g.iota(T.ia[:, 128:192], [[-16, 8], [0, 8]], 0, 1), "gi")
        gi["l"] = inc(g.iota(T.ia[:, 192:320], [[0, 16], [-16, 8]], 0, 1), "gi")
    for m, dsts in relay[f]:
        need("g", arrived(m))
        done = send(m, T.land[:, 128 * m:128 * m + 128], dsts, "rsent")

    tab1 = None
    if ta < 8192:
        need("y", done)
        tab1 = inc(g.sync.dma_start(T.tabs[:, ta:8192], T.tab[:, ta:8192]), "tab1", 16)

    G, GT, MQ = T.cst[:, 0:128], T.cst[:, 128:192], T.cst[:, 192:320]
    banks, win, later = [], {}, []

    def copy(q, ps, dst):
        if q == "s":
            return inc(g.scalar.activation(dst, ps, F.Copy), "s")
        return inc(V.tensor_copy(dst, ps), "v")

    def plane(w, m, part, q):
        hs = {"a": range(8), "l": range(4), "h": range(4, 8)}[part]
        k, n = len(banks) % NB, 64 * len(hs)
        need("p", arrived(m), c["ee"])
        if len(banks) >= NB:
            need("p", banks[-NB][0])
        ps, at = T["pw%d" % k], 512 * m + 64 * hs[0]
        col = 128 * m + (0 if w == "c" else 64)
        for x, h in enumerate(hs):
            t = inc(g.tensor.matmul(ps[:, 64 * x:64 * x + 64], T.ee[:, 128 * h:128 * h + 128],
                                    T.land[:, col:col + 64], True, True), "p")
        mine = [None]
        banks.append(mine)

        def out():
            need("v" if q == "w" else q, t)
            mine[0] = copy(q, ps[:, 0:n], T["w" + w][:, at:at + n])
            win.setdefault((m, w), []).append(mine[0])
        if q == "w":
            later.append(out)
        else:
            out()

    if chain:
        need("v", stl)
        a = inc(V.tensor_scalar(T.stk[:, :], T.sti[:, :], 15, None, A.bitwise_and), "v")
        b = inc(V.tensor_scalar(T.stc[:, :], T.sti[:, :], 4, None, A.arith_shift_right), "v")
        need("v", a)
        a = inc(V.tensor_copy(T.stkf[:, :], T.stk[:, :]), "v")
        need("v", b)
        off = inc(V.tensor_copy(T.off0[:, :], T.stc[:, :]), "v")
        need("v", a, c["dg"])
        for q in range(8):
            t = inc(V.tensor_scalar(T.x0[:, 16 * q:16 * q + 16], T.dg[:, 16 * q:16 * q + 16],
                                    T.stkf[:, q:q + 1], None, A.mult), "v")
        need("p", t, c["g"], c["nd"])
        t = inc(g.tensor.matmul(T.repk[:, 0:128], G, T.x0[:, :], True, True), "p")
        need("v", t, c["rc"])
        sel = inc(V.tensor_scalar(T.sel0[:, :], T.repk[:, 0:128], T.rc[:, 0:1], None, A.is_equal), "v")
        need("v", gi["l"])
        a = inc(V.tensor_scalar(T.ib[:, 128:320], T.ia[:, 128:320], 4, None, A.arith_shift_right), "v")
        need("v", a)
        c["cst"] = inc(V.tensor_scalar(T.cst[:, 128:320], T.ib[:, 128:320], 0.0, None, A.is_equal), "v")
        par, scan = 0, None
        for word in ORDER[f].split():
            m = int(word[1])
            if word[0] != "s":
                plane(word[0], m, word[2], word[3])
                continue
            xc, xk = T["xc%d" % par], T["xk%d" % par]
            offs, sl = T["off%d" % par][:, 0:8], T["sel%d" % par][:, :]
            need("v", off, sel, *win[(m, "c")])
            tc = inc(V.tensor_tensor(xc[:, :], T.wc[:, 512 * m:512 * m + 512].indirect(offs), sl, A.mult), "v")
            need("v", *win[(m, "k")])
            tk = inc(V.tensor_tensor(xk[:, :], T.wk[:, 512 * m:512 * m + 512].indirect(offs), sl, A.mult), "v")
            if m == f + 1:
                break
            need("p", scan)
            g.tensor.matmul(T.repc[:, 0:128], T.dg[0:16, :], T.nd[0:16, :], True, False)
            need("p", tc)
            rc_ = inc(g.tensor.matmul(T.repc[:, 0:128], G, xc[:, :], False, True), "p")
            need("p", tk)
            rk_ = inc(g.tensor.matmul(T.repk[:, 0:128], G, xk[:, :], True, True), "p")
            while later:
                later.pop(0)()
            zs, par = T["zs%d" % par], 1 - par
            need("v", rc_, c["rs"])
            scan = inc(V.tensor_tensor_scan(zs[:, :], T.rs[:, :], T.repc[:, 0:128], 0.0, A.add, A.max), "v")
            need("v", rk_)
            sel = inc(V.tensor_scalar(T["sel%d" % par][:, :], T.repk[:, 0:128], T.rc[:, 0:1], None, A.is_equal), "v")
            need("v", scan)
            off = inc(V.tensor_scalar(T["off%d" % par][:, :], zs[:, 15:128:16], 256.0, None, A.add), "v")
        need("p", tc, c["cst"])
        inc(g.tensor.matmul(T.repc[:, 0:64], xc[:, :], GT, True, True), "p")
        need("p", tk)
        t = inc(g.tensor.matmul(T.repc[:, 64:128], xk[:, :], GT, True, True), "p")
        need("v", t)
        t = inc(V.tensor_tensor(T.sp[:, :], T.repc[:, 0:128], MQ, A.mult), "v")
        need("p", t, c["dg16"])
        g.tensor.matmul(T.repk[:, 0:64], T.dg16[:, :], T.sp[:, 0:64], True, False)
        t = inc(g.tensor.matmul(T.repk[:, 0:64], T.dg[:, :], T.sp[:, 64:128], False, True), "p")
        need("v", t)
        t = inc(V.tensor_scalar(T.foff[:, :], T.repk[:, 0:64], 4096.0, None, A.add), "v")
    else:
        need("v", stl)
        t = inc(V.tensor_copy(T.foff[:, :], T.stf[:, :]), "v")

    need("v", t, tab0, tab1)
    need("s", t, tab0, tab1)
    pieces = [(0, 256, "v"), (512, 1024, "s"), (256, 512, "v")]
    toks = []
    for lo, hi, q in pieces:
        src = T.tabs[:, :].indirect(T.foff[:, lo // 16:hi // 16])
        toks.append(copy(q, src, T.yb[:, lo:hi]))
    for i in (0, 2, 1):
        lo, hi, q = pieces[i]
        need("s" if q == "s" else "y", toks[i])
        eng = g.scalar if q == "s" else g.sync
        inc(eng.dma_start(T.y[:, lo:hi], T.yb[:, lo:hi]), "y%d" % i, 16)

    for s in sorted(cnt):
        need("g", (s, cnt[s]))
    for m in range(f + 1, N):
        need("g", arrived(m))
